import numpy as np, ml_dtypes
CORES = [68,69,70,71,76,77,78,79,84,85,86,87]
N = 12
G1 = [0,1,2,3,4,5,6,7,8,9,10,11]
ROOT1 = 7
G2 = [0,1,2,3,8,9,10,11]
def setup_inputs(rng):
    return {"x1": rng.standard_normal((N, 128, 32), dtype=np.float32), "x2": rng.standard_normal((N, 128, 1024), dtype=np.float32).astype(ml_dtypes.bfloat16)}
def reference(x1, x2):
    out = {}
    y = np.full((N, 128, 384), np.nan, x1.dtype)
    y[G1[ROOT1]] = np.concatenate([x1[r] for r in G1], axis=1)
    out["y1"] = y
    y = np.full((N, 128, 1024), np.nan, x2.dtype)
    s = x2[G2].sum(axis=0, dtype=np.float64).astype(x2.dtype)
    for r in G2:
        y[r] = s
    out["y2"] = y
    return out

@@ -1,0 +1,193 @@
+from concourse.bass import DstId, RemoteDMATransfer
+
+MODE = "H2"
+K = 1
+PPC = 4 if MODE == "H" else 8
+P = PPC * K
+W = 1024 // P
+NSRC = 8 if MODE == "D" else 4
+
+SCRATCH = {
+    "xin": ("dram", [P, 128, W], "bfloat16"),
+    "res": ("dram", [P, 128, W], "bfloat16"),
+    "raw": ("dram", [K * NSRC, 128, W], "bfloat16"),
+    "braw": ("dram", [K * 4, 128, W], "bfloat16"),
+    "part": ("dram", [K * 3, 128, W], "bfloat16"),
+    "x1s": ("dram", [128, 32], "float32"),
+    "agg": ("sbuf", [128, 128], "float32"),
+    "land": ("sbuf", [128, 384], "float32"),
+}
+SEMAPHORES = ["ld1", "g1arr", "home", "far0", "far1", "st1", "st2", "sent"] + [
+    n + str(k) for k in range(K) for n in ("ld2_", "raw_", "braw_", "part_", "res_")]
+
+
+def rank_program(g, core, T, topo):
+    S = T.sem
+    tb = T.tables
+    chip = topo.chip
+    g1 = [T.cores[r] for r in tb["G1"]]
+    g2 = [T.cores[r] for r in tb["G2"]]
+    root = g1[tb["ROOT1"]]
+    ch = chip(core)
+    chips2 = sorted(set(chip(c) for c in g2))
+    mem = dict((c2, [c for c in g2 if chip(c) == c2]) for c2 in chips2)
+    hlp = dict((c2, [8 * c2 + j for j in range(4)]) for c2 in chips2)
+    allh = hlp[chips2[0]] + hlp[chips2[1]]
+    sent = [0]
+
+    def X(**kw):
+        sent[0] += bin(kw["dma_engine_mask"]).count("1")
+        return RemoteDMATransfer(**kw)
+
+    def dest(c):
+        rid, pid, _ = topo.addr(c)
+        return DstId(rid=rid, pnc=pid)
+
+    def fused(trs):
+        g.remote_dma_fused(trs, local_sem=S.sent)
+
+    def write(dst, out, in_, sem):
+        rid, pid, _ = topo.addr(dst)
+        mask = topo.mask(core, dst)
+        g.remote_dma(out, in_, sem, S.sent, pid, rid, mask)
+        sent[0] += bin(mask).count("1")
+
+    in1 = core in g1
+    if in1:
+        pos = g1.index(core)
+        cm = [c for c in g1 if chip(c) == ch]
+        base = g1.index(cm[0])
+        aggc = root if ch == chip(root) else cm[-1]
+        far = sorted(set(chip(c) for c in g1 if chip(c) != chip(root)))
+
+    def gather_load():
+        if not in1:
+            return
+        if core == root:
+            g.scalar.dma_start(T.land[:, 32 * pos:32 * pos + 32], T.x1[:]).then_inc(S.ld1, 16)
+        elif core == aggc:
+            g.scalar.dma_start(T.agg[:, 32 * (pos - base):32 * (pos - base) + 32], T.x1[:]).then_inc(S.ld1, 16)
+        else:
+            g.scalar.dma_start(T.x1s[:], T.x1[:]).then_inc(S.ld1, 16)
+
+    def gather_send():
+        if not in1 or core == aggc:
+            return
+        g.wait_ge(S.ld1, 16)
+        if aggc == root:
+            write(root, T.land[:, 32 * pos:32 * pos + 32], T.x1s[:], S.home)
+        else:
+            write(aggc, T.agg[:, 32 * (pos - base):32 * (pos - base) + 32], T.x1s[:], S.g1arr)
+
+    def gather_relay():
+        if not in1 or core != aggc or core == root:
+            return
+        g.wait_ge(S.ld1, 16)
+        g.wait_ge(S.g1arr, 16 * (len(cm) - 1))
+        write(root, T.land[:, 32 * base:32 * (base + len(cm))], T.agg[:], S["far%d" % far.index(ch)])
+
+    def gather_root():
+        if not in1 or core != root:
+            return
+        lo, hi = 32 * base, 32 * (base + len(cm))
+        g.sync.wait_ge(S.ld1, 16)
+        g.sync.wait_ge(S.home, 16 * (len(cm) - 1))
+        g.sync.dma_start(T.y1[:, lo:hi], T.land[:, lo:hi]).then_inc(S.st1, 16)
+        for i, fc in enumerate(far):
+            fm = [c for c in g1 if chip(c) == fc]
+            lo = 32 * g1.index(fm[0])
+            hi = lo + 32 * len(fm)
+            qu = g.scalar if i == 0 else g.sync
+            qu.wait_ge(S["far%d" % i], 8)
+            qu.dma_start(T.y1[:, lo:hi], T.land[:, lo:hi]).then_inc(S.st1, 16)
+        g.wait_ge(S.st1, 16 * (1 + len(far)))
+
+    if core in g2:
+        m = mem[ch].index(core)
+        och = [c for c in chips2 if c != ch][0]
+        rows = 128 // K
+        for k in range(K):
+            g.sync.dma_start(T.xin[k * PPC:(k + 1) * PPC], T.x2[k * rows:(k + 1) * rows, :]).then_inc(
+                S["ld2_%d" % k], 16)
+        gather_load()
+        for k in range(K):
+            g.wait_ge(S["ld2_%d" % k], 16)
+            trs = []
+            if MODE == "D":
+                non, noff = 0, 0
+                for e, h in enumerate(allh):
+                    if chip(h) == ch:
+                        mask = 0x3 << (8 + 2 * non)
+                        non += 1
+                    else:
+                        mask = 0x3 << (2 * noff)
+                        noff += 1
+                    trs.append(X(dst_ids=[dest(h)], dma_engine_mask=mask, remote_sem=S["raw_%d" % k],
+                                 src=T.xin[k * 8 + e], dst=T.raw[k * 8 + g2.index(core)]))
+            else:
+                ne = 4 if MODE == "H" else 2
+                n = 0
+                for q, h in enumerate(hlp[ch]):
+                    trs.append(X(dst_ids=[dest(h)], dma_engine_mask=((1 << ne) - 1) << (ne * n),
+                                 remote_sem=S["raw_%d" % k], src=T.xin[k * PPC + q], dst=T.raw[k * 4 + m]))
+                    n += 1
+                if MODE == "H2":
+                    for q, r in enumerate(mem[ch]):
+                        if r != core:
+                            trs.append(X(dst_ids=[dest(r)], dma_engine_mask=((1 << ne) - 1) << (ne * n),
+                                         remote_sem=S["braw_%d" % k], src=T.xin[k * 8 + 4 + q],
+                                         dst=T.braw[k * 4 + m]))
+                            n += 1
+            fused(trs)
+        gather_send()
+        if MODE == "H2":
+            for k in range(K):
+                g.wait_ge(S["braw_%d" % k], 2 * 3)
+                srcs = [T.xin[k * 8 + 4 + m] if i == m else T.braw[k * 4 + i] for i in range(4)]
+                fused([X(dst_ids=[dest(hlp[och][m])], dma_engine_mask=0x00FF, remote_sem=S["part_%d" % k],
+                         srcs=srcs, dsts=[T.part[k * 3 + 2]], alu_op=1),
+                       X(dst_ids=[dest(hlp[ch][m])], dma_engine_mask=0xFF00, remote_sem=S["part_%d" % k],
+                         srcs=srcs, dsts=[T.part[k * 3 + 1]], alu_op=1)])
+        gather_relay()
+        for k in range(K):
+            g.sync.wait_ge(S["res_%d" % k], 64)
+            g.sync.dma_start(T.y2[k * rows:(k + 1) * rows, :], T.res[k * PPC:(k + 1) * PPC]).then_inc(S.st2, 16)
+        g.sync.wait_ge(S.st2, 16 * K)
+    elif core in allh:
+        q = hlp[ch].index(core)
+        och = [c for c in chips2 if c != ch][0]
+        if MODE == "D":
+            e = allh.index(core)
+            for k in range(K):
+                g.wait_ge(S["raw_%d" % k], 16)
+                srcs = [T.raw[k * 8 + i] for i in range(8)]
+                fused([X(dst_ids=[dest(c) for c in mem[och]], dma_engine_mask=0x00FF, remote_sem=S["res_%d" % k],
+                         srcs=srcs, dsts=[T.res[k * 8 + e]] * 4, alu_op=1),
+                       X(dst_ids=[dest(c) for c in mem[ch]], dma_engine_mask=0xFF00, remote_sem=S["res_%d" % k],
+                         srcs=srcs, dsts=[T.res[k * 8 + e]] * 4, alu_op=1)])
+        else:
+            ne = 4 if MODE == "H" else 2
+            for k in range(K):
+                g.wait_ge(S["raw_%d" % k], 4 * ne)
+                fused([X(dst_ids=[dest(hlp[och][q])], dma_engine_mask=0x00FF, remote_sem=S["part_%d" % k],
+                         srcs=[T.raw[k * 4 + i] for i in range(4)], dsts=[T.part[k * 3]], alu_op=1)])
+            for k in range(K):
+                dsts = [dest(c) for c in mem[ch]]
+                srcs = [T.raw[k * 4 + i] for i in range(4)] + [T.part[k * 3]]
+                if MODE == "H":
+                    g.wait_ge(S["part_%d" % k], 8)
+                    fused([X(dst_ids=dsts, dma_engine_mask=0xFFFF, remote_sem=S["res_%d" % k],
+                             srcs=srcs, dsts=[T.res[k * 4 + q]] * 4, alu_op=1)])
+                else:
+                    g.wait_ge(S["part_%d" % k], 24)
+                    fused([X(dst_ids=dsts, dma_engine_mask=0x00FF, remote_sem=S["res_%d" % k],
+                             srcs=srcs, dsts=[T.res[k * 8 + q]] * 4, alu_op=1),
+                           X(dst_ids=dsts, dma_engine_mask=0xFF00, remote_sem=S["res_%d" % k],
+                             srcs=[T.part[k * 3 + 1], T.part[k * 3 + 2]], dsts=[T.res[k * 8 + 4 + q]] * 4,
+                             alu_op=1)])
+    elif in1:
+        gather_load()
+        gather_send()
+        gather_root()
+    if sent[0]:
+        g.wait_ge(S.sent, sent[0])

@@ -1,16 +1,13 @@
 from concourse.bass import DstId, RemoteDMATransfer
 
-MODE = "H2"
-K = 1
-PPC = 4 if MODE == "H" else 8
-P = PPC * K
+K = 2
+P = 8 * K
 W = 1024 // P
-NSRC = 8 if MODE == "D" else 4
 
 SCRATCH = {
     "xin": ("dram", [P, 128, W], "bfloat16"),
     "res": ("dram", [P, 128, W], "bfloat16"),
-    "raw": ("dram", [K * NSRC, 128, W], "bfloat16"),
+    "raw": ("dram", [K * 4, 128, W], "bfloat16"),
     "braw": ("dram", [K * 4, 128, W], "bfloat16"),
     "part": ("dram", [K * 3, 128, W], "bfloat16"),
     "x1s": ("dram", [128, 32], "float32"),
@@ -61,8 +58,6 @@ def rank_program(g, core, T, topo):
         far = sorted(set(chip(c) for c in g1 if chip(c) != chip(root)))
 
     def gather_load():
-        if not in1:
-            return
         if core == root:
             g.scalar.dma_start(T.land[:, 32 * pos:32 * pos + 32], T.x1[:]).then_inc(S.ld1, 16)
         elif core == aggc:
@@ -71,7 +66,7 @@ def rank_program(g, core, T, topo):
             g.scalar.dma_start(T.x1s[:], T.x1[:]).then_inc(S.ld1, 16)
 
     def gather_send():
-        if not in1 or core == aggc:
+        if core == aggc:
             return
         g.wait_ge(S.ld1, 16)
         if aggc == root:
@@ -80,14 +75,14 @@ def rank_program(g, core, T, topo):
             write(aggc, T.agg[:, 32 * (pos - base):32 * (pos - base) + 32], T.x1s[:], S.g1arr)
 
     def gather_relay():
-        if not in1 or core != aggc or core == root:
+        if core != aggc or core == root:
             return
         g.wait_ge(S.ld1, 16)
         g.wait_ge(S.g1arr, 16 * (len(cm) - 1))
         write(root, T.land[:, 32 * base:32 * (base + len(cm))], T.agg[:], S["far%d" % far.index(ch)])
 
     def gather_root():
-        if not in1 or core != root:
+        if core != root:
             return
         lo, hi = 32 * base, 32 * (base + len(cm))
         g.sync.wait_ge(S.ld1, 16)
@@ -107,84 +102,49 @@ def rank_program(g, core, T, topo):
         och = [c for c in chips2 if c != ch][0]
         rows = 128 // K
         for k in range(K):
-            g.sync.dma_start(T.xin[k * PPC:(k + 1) * PPC], T.x2[k * rows:(k + 1) * rows, :]).then_inc(
+            g.sync.dma_start(T.xin[k * 8:(k + 1) * 8], T.x2[k * rows:(k + 1) * rows, :]).then_inc(
                 S["ld2_%d" % k], 16)
         gather_load()
         for k in range(K):
             g.wait_ge(S["ld2_%d" % k], 16)
             trs = []
-            if MODE == "D":
-                non, noff = 0, 0
-                for e, h in enumerate(allh):
-                    if chip(h) == ch:
-                        mask = 0x3 << (8 + 2 * non)
-                        non += 1
-                    else:
-                        mask = 0x3 << (2 * noff)
-                        noff += 1
-                    trs.append(X(dst_ids=[dest(h)], dma_engine_mask=mask, remote_sem=S["raw_%d" % k],
-                                 src=T.xin[k * 8 + e], dst=T.raw[k * 8 + g2.index(core)]))
-            else:
-                ne = 4 if MODE == "H" else 2
-                n = 0
-                for q, h in enumerate(hlp[ch]):
-                    trs.append(X(dst_ids=[dest(h)], dma_engine_mask=((1 << ne) - 1) << (ne * n),
-                                 remote_sem=S["raw_%d" % k], src=T.xin[k * PPC + q], dst=T.raw[k * 4 + m]))
-                    n += 1
-                if MODE == "H2":
-                    for q, r in enumerate(mem[ch]):
-                        if r != core:
-                            trs.append(X(dst_ids=[dest(r)], dma_engine_mask=((1 << ne) - 1) << (ne * n),
-                                         remote_sem=S["braw_%d" % k], src=T.xin[k * 8 + 4 + q],
-                                         dst=T.braw[k * 4 + m]))
-                            n += 1
+            for q, h in enumerate(hlp[ch]):
+                trs.append(X(dst_ids=[dest(h)], dma_engine_mask=0x3 << (2 * len(trs)),
+                             remote_sem=S["raw_%d" % k], src=T.xin[k * 8 + q], dst=T.raw[k * 4 + m]))
+            for q, r in enumerate(mem[ch]):
+                if r != core:
+                    trs.append(X(dst_ids=[dest(r)], dma_engine_mask=0x3 << (2 * len(trs)),
+                                 remote_sem=S["braw_%d" % k], src=T.xin[k * 8 + 4 + q], dst=T.braw[k * 4 + m]))
             fused(trs)
         gather_send()
-        if MODE == "H2":
-            for k in range(K):
-                g.wait_ge(S["braw_%d" % k], 2 * 3)
-                srcs = [T.xin[k * 8 + 4 + m] if i == m else T.braw[k * 4 + i] for i in range(4)]
-                fused([X(dst_ids=[dest(hlp[och][m])], dma_engine_mask=0x00FF, remote_sem=S["part_%d" % k],
-                         srcs=srcs, dsts=[T.part[k * 3 + 2]], alu_op=1),
-                       X(dst_ids=[dest(hlp[ch][m])], dma_engine_mask=0xFF00, remote_sem=S["part_%d" % k],
-                         srcs=srcs, dsts=[T.part[k * 3 + 1]], alu_op=1)])
+        for k in range(K):
+            g.wait_ge(S["braw_%d" % k], 2 * 3)
+            srcs = [T.xin[k * 8 + 4 + m] if i == m else T.braw[k * 4 + i] for i in range(4)]
+            fused([X(dst_ids=[dest(hlp[och][m])], dma_engine_mask=0x00FF, remote_sem=S["part_%d" % k],
+                     srcs=srcs, dsts=[T.part[k * 3 + 2]], alu_op=1),
+                   X(dst_ids=[dest(hlp[ch][m])], dma_engine_mask=0xFF00, remote_sem=S["part_%d" % k],
+                     srcs=srcs, dsts=[T.part[k * 3 + 1]], alu_op=1)])
         gather_relay()
         for k in range(K):
-            g.sync.wait_ge(S["res_%d" % k], 64)
-            g.sync.dma_start(T.y2[k * rows:(k + 1) * rows, :], T.res[k * PPC:(k + 1) * PPC]).then_inc(S.st2, 16)
-        g.sync.wait_ge(S.st2, 16 * K)
+            qu = g.scalar if k % 2 else g.sync
+            qu.wait_ge(S["res_%d" % k], 64)
+            qu.dma_start(T.y2[k * rows:(k + 1) * rows, :], T.res[k * 8:(k + 1) * 8]).then_inc(S.st2, 16)
+        g.wait_ge(S.st2, 16 * K)
     elif core in allh:
         q = hlp[ch].index(core)
         och = [c for c in chips2 if c != ch][0]
-        if MODE == "D":
-            e = allh.index(core)
-            for k in range(K):
-                g.wait_ge(S["raw_%d" % k], 16)
-                srcs = [T.raw[k * 8 + i] for i in range(8)]
-                fused([X(dst_ids=[dest(c) for c in mem[och]], dma_engine_mask=0x00FF, remote_sem=S["res_%d" % k],
-                         srcs=srcs, dsts=[T.res[k * 8 + e]] * 4, alu_op=1),
-                       X(dst_ids=[dest(c) for c in mem[ch]], dma_engine_mask=0xFF00, remote_sem=S["res_%d" % k],
-                         srcs=srcs, dsts=[T.res[k * 8 + e]] * 4, alu_op=1)])
-        else:
-            ne = 4 if MODE == "H" else 2
-            for k in range(K):
-                g.wait_ge(S["raw_%d" % k], 4 * ne)
-                fused([X(dst_ids=[dest(hlp[och][q])], dma_engine_mask=0x00FF, remote_sem=S["part_%d" % k],
-                         srcs=[T.raw[k * 4 + i] for i in range(4)], dsts=[T.part[k * 3]], alu_op=1)])
-            for k in range(K):
-                dsts = [dest(c) for c in mem[ch]]
-                srcs = [T.raw[k * 4 + i] for i in range(4)] + [T.part[k * 3]]
-                if MODE == "H":
-                    g.wait_ge(S["part_%d" % k], 8)
-                    fused([X(dst_ids=dsts, dma_engine_mask=0xFFFF, remote_sem=S["res_%d" % k],
-                             srcs=srcs, dsts=[T.res[k * 4 + q]] * 4, alu_op=1)])
-                else:
-                    g.wait_ge(S["part_%d" % k], 24)
-                    fused([X(dst_ids=dsts, dma_engine_mask=0x00FF, remote_sem=S["res_%d" % k],
-                             srcs=srcs, dsts=[T.res[k * 8 + q]] * 4, alu_op=1),
-                           X(dst_ids=dsts, dma_engine_mask=0xFF00, remote_sem=S["res_%d" % k],
-                             srcs=[T.part[k * 3 + 1], T.part[k * 3 + 2]], dsts=[T.res[k * 8 + 4 + q]] * 4,
-                             alu_op=1)])
+        for k in range(K):
+            g.wait_ge(S["raw_%d" % k], 2 * 4)
+            fused([X(dst_ids=[dest(hlp[och][q])], dma_engine_mask=0x00FF, remote_sem=S["part_%d" % k],
+                     srcs=[T.raw[k * 4 + i] for i in range(4)], dsts=[T.part[k * 3]], alu_op=1)])
+        for k in range(K):
+            dsts = [dest(c) for c in mem[ch]]
+            g.wait_ge(S["part_%d" % k], 24)
+            fused([X(dst_ids=dsts, dma_engine_mask=0x00FF, remote_sem=S["res_%d" % k],
+                     srcs=[T.raw[k * 4 + i] for i in range(4)] + [T.part[k * 3]],
+                     dsts=[T.res[k * 8 + q]] * 4, alu_op=1),
+                   X(dst_ids=dsts, dma_engine_mask=0xFF00, remote_sem=S["res_%d" % k],
+                     srcs=[T.part[k * 3 + 1], T.part[k * 3 + 2]], dsts=[T.res[k * 8 + 4 + q]] * 4, alu_op=1)])
     elif in1:
         gather_load()
         gather_send()

from concourse.bass import DstId, RemoteDMATransfer

K = 2
P = 8 * K
W = 1024 // P

SCRATCH = {
    "xin": ("dram", [P, 128, W], "bfloat16"),
    "res": ("dram", [P, 128, W], "bfloat16"),
    "raw": ("dram", [K * 4, 128, W], "bfloat16"),
    "braw": ("dram", [K * 4, 128, W], "bfloat16"),
    "part": ("dram", [K * 3, 128, W], "bfloat16"),
    "x1s": ("dram", [128, 32], "float32"),
    "agg": ("sbuf", [128, 128], "float32"),
    "land": ("sbuf", [128, 384], "float32"),
}
SEMAPHORES = ["ld1", "g1arr", "home", "far0", "far1", "st1", "st2", "sent"] + [
    n + str(k) for k in range(K) for n in ("ld2_", "raw_", "braw_", "part_", "res_")]


def rank_program(g, core, T, topo):
    S = T.sem
    tb = T.tables
    chip = topo.chip
    g1 = [T.cores[r] for r in tb["G1"]]
    g2 = [T.cores[r] for r in tb["G2"]]
    root = g1[tb["ROOT1"]]
    ch = chip(core)
    chips2 = sorted(set(chip(c) for c in g2))
    mem = dict((c2, [c for c in g2 if chip(c) == c2]) for c2 in chips2)
    hlp = dict((c2, [8 * c2 + j for j in range(4)]) for c2 in chips2)
    allh = hlp[chips2[0]] + hlp[chips2[1]]
    sent = [0]

    def X(**kw):
        sent[0] += bin(kw["dma_engine_mask"]).count("1")
        return RemoteDMATransfer(**kw)

    def dest(c):
        rid, pid, _ = topo.addr(c)
        return DstId(rid=rid, pnc=pid)

    def fused(trs):
        g.remote_dma_fused(trs, local_sem=S.sent)

    def write(dst, out, in_, sem):
        rid, pid, _ = topo.addr(dst)
        mask = topo.mask(core, dst)
        g.remote_dma(out, in_, sem, S.sent, pid, rid, mask)
        sent[0] += bin(mask).count("1")

    in1 = core in g1
    if in1:
        pos = g1.index(core)
        cm = [c for c in g1 if chip(c) == ch]
        base = g1.index(cm[0])
        aggc = root if ch == chip(root) else cm[-1]
        far = sorted(set(chip(c) for c in g1 if chip(c) != chip(root)))

    def gather_load():
        if core == root:
            g.scalar.dma_start(T.land[:, 32 * pos:32 * pos + 32], T.x1[:]).then_inc(S.ld1, 16)
        elif core == aggc:
            g.scalar.dma_start(T.agg[:, 32 * (pos - base):32 * (pos - base) + 32], T.x1[:]).then_inc(S.ld1, 16)
        else:
            g.scalar.dma_start(T.x1s[:], T.x1[:]).then_inc(S.ld1, 16)

    def gather_send():
        if core == aggc:
            return
        g.wait_ge(S.ld1, 16)
        if aggc == root:
            write(root, T.land[:, 32 * pos:32 * pos + 32], T.x1s[:], S.home)
        else:
            write(aggc, T.agg[:, 32 * (pos - base):32 * (pos - base) + 32], T.x1s[:], S.g1arr)

    def gather_relay():
        if core != aggc or core == root:
            return
        g.wait_ge(S.ld1, 16)
        g.wait_ge(S.g1arr, 16 * (len(cm) - 1))
        write(root, T.land[:, 32 * base:32 * (base + len(cm))], T.agg[:], S["far%d" % far.index(ch)])

    def gather_root():
        if core != root:
            return
        lo, hi = 32 * base, 32 * (base + len(cm))
        g.sync.wait_ge(S.ld1, 16)
        g.sync.wait_ge(S.home, 16 * (len(cm) - 1))
        g.sync.dma_start(T.y1[:, lo:hi], T.land[:, lo:hi]).then_inc(S.st1, 16)
        for i, fc in enumerate(far):
            fm = [c for c in g1 if chip(c) == fc]
            lo = 32 * g1.index(fm[0])
            hi = lo + 32 * len(fm)
            qu = g.scalar if i == 0 else g.sync
            qu.wait_ge(S["far%d" % i], 8)
            qu.dma_start(T.y1[:, lo:hi], T.land[:, lo:hi]).then_inc(S.st1, 16)
        g.wait_ge(S.st1, 16 * (1 + len(far)))

    if core in g2:
        m = mem[ch].index(core)
        och = [c for c in chips2 if c != ch][0]
        rows = 128 // K
        for k in range(K):
            g.sync.dma_start(T.xin[k * 8:(k + 1) * 8], T.x2[k * rows:(k + 1) * rows, :]).then_inc(
                S["ld2_%d" % k], 16)
        gather_load()
        for k in range(K):
            g.wait_ge(S["ld2_%d" % k], 16)
            trs = []
            for q, h in enumerate(hlp[ch]):
                trs.append(X(dst_ids=[dest(h)], dma_engine_mask=0x3 << (2 * len(trs)),
                             remote_sem=S["raw_%d" % k], src=T.xin[k * 8 + q], dst=T.raw[k * 4 + m]))
            for q, r in enumerate(mem[ch]):
                if r != core:
                    trs.append(X(dst_ids=[dest(r)], dma_engine_mask=0x3 << (2 * len(trs)),
                                 remote_sem=S["braw_%d" % k], src=T.xin[k * 8 + 4 + q], dst=T.braw[k * 4 + m]))
            fused(trs)
        gather_send()
        for k in range(K):
            g.wait_ge(S["braw_%d" % k], 2 * 3)
            srcs = [T.xin[k * 8 + 4 + m] if i == m else T.braw[k * 4 + i] for i in range(4)]
            fused([X(dst_ids=[dest(hlp[och][m])], dma_engine_mask=0x00FF, remote_sem=S["part_%d" % k],
                     srcs=srcs, dsts=[T.part[k * 3 + 2]], alu_op=1),
                   X(dst_ids=[dest(hlp[ch][m])], dma_engine_mask=0xFF00, remote_sem=S["part_%d" % k],
                     srcs=srcs, dsts=[T.part[k * 3 + 1]], alu_op=1)])
        gather_relay()
        for k in range(K):
            qu = g.scalar if k % 2 else g.sync
            qu.wait_ge(S["res_%d" % k], 64)
            qu.dma_start(T.y2[k * rows:(k + 1) * rows, :], T.res[k * 8:(k + 1) * 8]).then_inc(S.st2, 16)
        g.wait_ge(S.st2, 16 * K)
    elif core in allh:
        q = hlp[ch].index(core)
        och = [c for c in chips2 if c != ch][0]
        for k in range(K):
            g.wait_ge(S["raw_%d" % k], 2 * 4)
            fused([X(dst_ids=[dest(hlp[och][q])], dma_engine_mask=0x00FF, remote_sem=S["part_%d" % k],
                     srcs=[T.raw[k * 4 + i] for i in range(4)], dsts=[T.part[k * 3]], alu_op=1)])
        for k in range(K):
            dsts = [dest(c) for c in mem[ch]]
            g.wait_ge(S["part_%d" % k], 24)
            fused([X(dst_ids=dsts, dma_engine_mask=0x00FF, remote_sem=S["res_%d" % k],
                     srcs=[T.raw[k * 4 + i] for i in range(4)] + [T.part[k * 3]],
                     dsts=[T.res[k * 8 + q]] * 4, alu_op=1),
                   X(dst_ids=dsts, dma_engine_mask=0xFF00, remote_sem=S["res_%d" % k],
                     srcs=[T.part[k * 3 + 1], T.part[k * 3 + 2]], dsts=[T.res[k * 8 + 4 + q]] * 4, alu_op=1)])
    elif in1:
        gather_load()
        gather_send()
        gather_root()
    if sent[0]:
        g.wait_ge(S.sent, sent[0])
